import numpy as np
import ml_dtypes


def mxq(x, axis, fmt="e4m3"):
    dtype, down = {"e4m3": (ml_dtypes.float8_e4m3fn, 7), "e5m2": (ml_dtypes.float8_e5m2, 14)}[fmt]
    v = np.moveaxis(np.asarray(x, np.float32).astype(ml_dtypes.bfloat16).astype(np.float64), axis, -1)
    blocks = v.reshape(v.shape[:-1] + (-1, 32))
    amax = np.abs(blocks).max(-1, keepdims=True)
    byte = np.maximum(np.where(amax > 0, np.frexp(amax)[1] - 1 + 127, 0) - down, 1)
    scale = np.exp2(byte - 127.0)
    codes = (blocks / scale).astype(np.float32).astype(dtype).astype(np.float64)
    return np.moveaxis((codes * scale).reshape(v.shape), -1, axis)


WIDE = False


def mx_kscale(k):
    if not WIDE:
        return np.ones(k)
    levels = np.array([10, -10, 5, -5, 0])
    if k % 512:
        return np.exp2(np.random.permutation(np.resize(levels, k // 32))).repeat(32)
    a = np.empty((k // 512, 16))
    for p in range(k // 512):
        a[p, :8] = np.random.permutation(np.resize(levels, 8))
        for g in range(8):
            far = levels[np.abs(levels - a[p, g]) >= 10]
            a[p, g + 8] = far[np.random.randint(len(far))]
    return np.exp2(a.ravel()).repeat(32)


def f64(x):
    return np.asarray(x).astype(np.float64)


def striped(idx):
    return np.tile(idx.reshape(-1, 16).T, (8, 1)).astype(np.uint16)


def unstriped(offs):
    return offs[:16].T.reshape(-1).astype(np.int64)


E2M1 = np.array([0.0, 0.5, 1.0, 1.5, 2.0, 3.0, 4.0, 6.0, -0.0, -0.5, -1.0, -1.5, -2.0, -3.0, -4.0, -6.0])


def pack_weight(w, fmt):
    k, n = w.shape
    w = f64(np.asarray(w, np.float32).astype(ml_dtypes.bfloat16)).reshape(k // 32, 32, n)
    amax = np.abs(w).max(1)
    if fmt == "e4m3":
        byte = np.frexp(amax)[1] - 1 + 127 - 7
    else:
        mant, ex = np.frexp(amax / 6.0)
        byte = np.where(mant > 0.5, ex, ex - 1) + 127
    byte = np.clip(np.where(amax > 0, byte, 1), 1, 254)
    scaled = (w * np.exp2(127.0 - byte)[:, None, :]).reshape(k, n).astype(np.float32)
    by_word = np.ascontiguousarray(scaled.reshape(k // 512, 128, 4, n).transpose(0, 1, 3, 2))
    if fmt == "e4m3":
        words = by_word.astype(ml_dtypes.float8_e4m3fn).view(np.uint8)
    else:
        c = by_word.astype(ml_dtypes.float4_e2m1fn).view(np.uint8) & 0xF
        words = (c[..., 0::2] | (c[..., 1::2] << 4)).reshape(k // 512, 128, 2 * n)
    return np.ascontiguousarray(words), np.ascontiguousarray(byte.astype(np.uint8).reshape(k // 512, 16, n))


def unpack_weight(words, scales, fmt):
    g, _, n = scales.shape
    words = np.ascontiguousarray(words).reshape(g, 128, n, -1)
    if fmt == "e4m3":
        vals = words.view(ml_dtypes.float8_e4m3fn).astype(np.float64)
    else:
        nib = np.empty((g, 128, n, 4), np.uint8)
        nib[..., 0::2] = words & 0xF
        nib[..., 1::2] = words >> 4
        vals = E2M1[nib]
    vals = vals * np.repeat(np.exp2(scales.astype(np.float64) - 127.0), 8, axis=1)[..., None]
    return vals.transpose(0, 1, 3, 2).reshape(g * 512, n)


def gelu(v):
    return 0.5 * v * (1.0 + np.tanh(np.sqrt(2.0 / np.pi) * (v + 0.044715 * v**3)))


K, H, N, T, S, P, P2 = 1024, 1024, 512, 4096, 1024, 512, 256

def setup_inputs():
    n = np.random.standard_normal
    s = mx_kscale(K)[:, None]
    u = mx_kscale(H)[:, None]
    d = {}
    d["tab_words"], d["tab_scales"] = pack_weight(n((K, T)) * s, "e4m3")
    d["offs"] = striped(np.random.permutation(T)[:S])
    d["pos1"] = striped(np.random.permutation(S)[:P])
    d["pos2"] = striped(np.random.permutation(P)[:P2])
    d["w1"] = (n((K, H)) / K**0.5 / s * u.T).astype(np.float32)
    d["low"] = (0.7 * n(H) * u[:, 0]).astype(np.float32)
    d["w2_words"], d["w2_scales"] = pack_weight(1.5 * n((H, H)) / H**0.5 / u, "e2m1")
    d["base"] = (0.8 * n((H, P))).astype(np.float32)
    d["gain"] = (np.random.uniform(0.7, 1.6, H) * u[:, 0]).astype(np.float32)
    d["w3"] = (0.7 * n((H, N)) / H**0.5 / u).astype(np.float32)
    d["w4_words"], d["w4_scales"] = pack_weight(0.8 * n((H, N)) / H**0.5 / u, "e4m3")
    return d

def reference(tab_words, tab_scales, offs, pos1, pos2, w1, low, w2_words, w2_scales, base, gain, w3, w4_words, w4_scales):
    v = unpack_weight(tab_words, tab_scales, "e4m3")[:, unstriped(offs)]
    w2 = unpack_weight(w2_words, w2_scales, "e2m1")
    w4 = unpack_weight(w4_words, w4_scales, "e4m3")
    h = np.maximum(mxq(f64(w1), 0, "e4m3").T @ v, f64(low)[:, None])
    x1 = h[:, unstriped(pos1)]
    t = np.tanh((w2.T @ mxq(x1, 0, "e4m3")) - f64(base))
    x2 = x1 + f64(gain)[:, None] * t
    x3 = mxq(x2[:, unstriped(pos2)], 0, "e4m3")
    y1 = mxq(f64(w3), 0, "e4m3").T @ x3
    y2 = w4.T @ x3
    return np.square(y1) + y2

@@ -1,0 +1,311 @@
+from contextlib import ExitStack
+
+import concourse.mybir as mybir
+
+K, H, N, T, S, P1, P2 = 1024, 1024, 512, 4096, 1024, 512, 256
+FLOPS = 2 * (K * H * S + H * H * P1 + 2 * H * N * P2)
+
+F32 = mybir.dt.float32
+BF16 = mybir.dt.bfloat16
+I32 = mybir.dt.int32
+U32 = mybir.dt.uint32
+U16 = mybir.dt.uint16
+U8 = mybir.dt.uint8
+E4M3 = mybir.dt.float8_e4m3fn_x4
+E2M1 = mybir.dt.float4_e2m1fn_x4
+ALU = mybir.AluOpType
+ACT = mybir.ActivationFunctionType
+
+P = 128
+PACK = 4
+PASS = P * PACK
+PASSES = 2
+BANK = 512
+
+
+def tile_list_rope_trace_trunk_kernel(
+    tc, tab_words, tab_scales, offs, pos1, pos2, w1, low, w2_words, w2_scales, base, gain, w3, w4_words, w4_scales, out
+):
+    nc = tc.nc
+    with ExitStack() as ctx:
+        sb = ctx.enter_context(tc.tile_pool(name="sb", bufs=1))
+        ps = ctx.enter_context(tc.psum_pool(name="ps", bufs=1))
+
+        def tile(name, shape, dtype, tag=None):
+            return sb.tile(shape, dtype, name=name, tag=tag or name, align_bytes=64)
+
+        banks = [ps.tile([P, BANK], F32, name="bank%d" % i) for i in range(8)]
+
+        offs_sb = sb.tile([P, S // 16], U16, name="offs_sb")
+        pos1_sb = sb.tile([P, P1 // 16], U16, name="pos1_sb")
+        pos2_sb = sb.tile([P, P2 // 16], U16, name="pos2_sb")
+
+        tabw = [tile("tabw%d" % a, [P, T], U32) for a in range(PASSES)]
+        tabs = tile("tabs", [P, T], U8)
+        vw = [[tile("vw0%d" % f, [P, BANK], U32) for f in range(2)]]
+        vs = tile("vs", [P, S], U8)
+        raw = [[tile("raw%d%d" % (i, f), [P, PACK, 256], F32) for f in range(2)] for i in range(4)]
+        wbf = [tile("wbf%d" % i, [P, PASS * PACK], BF16) for i in range(2)]
+        w1c = [[tile("w1c%d%d" % (b, a), [P, PASS], U32) for a in range(PASSES)] for b in range(2)]
+        w1s = [[tile("w1s%d%d" % (b, a), [P, PASS], U8) for a in range(PASSES)] for b in range(2)]
+        h = [tile("h%d" % t, [P, S], F32) for t in range(PACK)]
+        x1 = [tile("x1_%d" % b, [P, PACK, P1], F32) for b in range(2)]
+        x1bf = [tile("x1bf%d" % b, [P, P1 * PACK], BF16) for b in range(2)]
+        x1c = [tile("x1c%d" % b, [P, P1], U32) for b in range(2)]
+        x1s = [tile("x1s%d" % b, [P, P1], U8) for b in range(2)]
+        w2raw = [tile("w2raw%d" % a, [P, H], U16) for a in range(PASSES)]
+        w2sraw = tile("w2sraw", [P, PASSES * H], U8)
+        base_sb = [tile("base%d" % b, [P, PACK, P1], F32) for b in range(2)]
+        low_sb = tile("low_sb", [P, 2, 8], F32)
+        gain_sb = tile("gain_sb", [P, 2, 8], F32)
+        z = [tile("z%d" % i, [P, P1], F32) for i in range(4)]
+        x2 = [tile("x2_%d" % i, [P, P1], F32) for i in range(2)]
+        x3 = [tile("x3_%d" % b, [P, PACK, P2], F32) for b in range(2)]
+        x3bf = [tile("x3bf%d" % b, [P, P2 * PACK], BF16) for b in range(2)]
+        x3c = [tile("x3c%d" % b, [P, P2], U32) for b in range(2)]
+        x3s = [tile("x3s%d" % b, [P, P2], U8) for b in range(2)]
+        w3c = [tile("w3c%d" % a, [P, N], U32) for a in range(PASSES)]
+        w3s = [tile("w3s%d" % a, [P, N], U8) for a in range(PASSES)]
+        w4c = tile("w4c", [P, PASSES, N], U32)
+        w4s = tile("w4s", [P, PASSES * N], U8)
+        sq = [tile("sq%d" % i, [P, P2], F32) for i in range(4)]
+        res = [tile("res%d" % i, [P, P2], F32) for i in range(4)]
+        warm = tile("warm", [P, 8], F32)
+
+        nc.vector.memset(tabs[:].bitcast(I32), 0)
+        nc.vector.memset(warm[:], 0.0)
+        nc.scalar.activation(warm[:, 0:1], warm[:, 4:5], ACT.Tanh)
+        nc.vector.memset(w2sraw[:].bitcast(I32), 0)
+        nc.vector.memset(w4s[:].bitcast(I32), 0)
+        for q in range(4):
+            nc.gpsimd.dma_start(
+                out=tabs[32 * q : 32 * q + 8, :].bitcast(I32), in_=tab_scales[:, 4 * q : 4 * q + 4, :].bitcast(I32)
+            )
+
+        def load_table(a):
+            nc.sync.dma_start(
+                out=tabw[a][:].bitcast(I32), in_=tab_words[a].rearrange("p t i -> p (t i)").bitcast(I32)
+            )
+
+        def load_weight(w, slot, a, c0):
+            for f in range(2):
+                cols = slice(c0 + 256 * f, c0 + 256 * (f + 1))
+                nc.sync.dma_start(
+                    out=raw[slot][f][:],
+                    in_=w[PASS * a : PASS * (a + 1), cols].rearrange("(p j) c -> p j c", j=PACK),
+                )
+
+        def load_vector(dst, vec):
+            nc.sync.dma_start(out=dst[:, :, 0:PACK], in_=vec.rearrange("(b p t) -> p b t", p=P, t=PACK))
+
+        nc.sync.dma_start(offs_sb[:], offs)
+        load_table(0)
+        load_weight(w1, 0, 0, 0)
+        load_table(1)
+        load_weight(w1, 1, 1, 0)
+        nc.sync.dma_start(pos1_sb[:], pos1)
+        load_vector(low_sb, low)
+        load_weight(w1, 2, 0, PASS)
+        load_weight(w1, 3, 1, PASS)
+        for a in range(PASSES):
+            nc.sync.dma_start(out=w2raw[a][:].bitcast(I32), in_=w2_words[a].bitcast(I32))
+        for q in range(4):
+            nc.sync.dma_start(
+                out=w2sraw[32 * q : 32 * q + 4, :].bitcast(I32).rearrange("r (a c) -> r a c", a=PASSES),
+                in_=w2_scales[:, 4 * q : 4 * q + 4, :].bitcast(I32).rearrange("a r c -> r a c"),
+            )
+        load_vector(gain_sb, gain)
+        nc.sync.dma_start(pos2_sb[:], pos2)
+        for b in range(2):
+            nc.sync.dma_start(
+                out=base_sb[b][:], in_=base[PASS * b : PASS * (b + 1), :].rearrange("(p t) j -> p t j", t=PACK)
+            )
+
+        def copy_on(engine, dst, src):
+            if engine == "vector":
+                nc.vector.tensor_copy(out=dst, in_=src)
+            else:
+                nc.scalar.copy(out=dst, in_=src)
+
+        def round_w1(slot, stage, engines):
+            dealt = wbf[stage][:].rearrange("p (t m j) -> p m j t", t=PACK, j=PACK)
+            for f in range(2):
+                copy_on(
+                    engines[f],
+                    dealt[:, 64 * f : 64 * (f + 1)],
+                    raw[slot][f][:].rearrange("p j (m t) -> p m j t", t=PACK),
+                )
+
+        def weave(engine, dst, src):
+            copy_on(
+                engine,
+                dst.rearrange("p (c i t) -> p c t i", i=4, t=PACK),
+                src.rearrange("p t (c i) -> p c t i", i=4),
+            )
+
+        def quantize(codes, scales, src, pieces=1):
+            width = codes.shape[1] // pieces
+            for i in range(pieces):
+                cols = slice(i * width, (i + 1) * width)
+                nc.vector.quantize_mx(
+                    out=codes[:, cols].bitcast(E4M3),
+                    scales=scales[:, cols],
+                    in_=src[:, PACK * i * width : PACK * (i + 1) * width],
+                )
+
+        def gather_table(a):
+            for f in range(2):
+                nc.vector.tensor_copy(vw[a][f][:], tabw[a][:].indirect(offs_sb[:, 32 * f : 32 * (f + 1)]))
+
+        def first_product(b, a):
+            for t in range(PACK):
+                cols = slice(P * t, P * (t + 1))
+                for f in range(2):
+                    nc.tensor.matmul_mx(
+                        out=banks[2 * t + f][:],
+                        lhsT=w1c[b][a][:, cols].bitcast(E4M3),
+                        lhsT_scale=w1s[b][a][:, cols],
+                        rhs=vw[a][f][:].bitcast(E4M3),
+                        rhs_scale=vs[4 * a : P, BANK * f : BANK * (f + 1)],
+                        start=(a == 0),
+                        stop=(a == PASSES - 1),
+                    )
+
+        def evacuate_h(t):
+            for f in range(2):
+                nc.scalar.copy(out=h[t][:, BANK * f : BANK * (f + 1)], in_=banks[2 * t + f][:])
+
+        def pick_x1(b, t):
+            nc.vector.tensor_copy(x1[b][:, t, :], h[t][:].indirect(pos1_sb[:]))
+
+        def floor_x1(b, t):
+            nc.vector.tensor_scalar(
+                out=x1[b][:, t, :], in0=x1[b][:, t, :], scalar1=low_sb[:, b, t : t + 1], scalar2=None, op0=ALU.max
+            )
+
+        def features(b):
+            for t in range(PACK):
+                evacuate_h(t)
+                pick_x1(b, t)
+                if t > 0:
+                    floor_x1(b, t - 1)
+            floor_x1(b, PACK - 1)
+
+        gather_table(0)
+        round_w1(0, 0, ("scalar", "scalar"))
+        nc.vector.tensor_copy(vs[:], tabs[:].indirect(offs_sb[:]))
+        quantize(w1c[0][0], w1s[0][0], wbf[0])
+        first_product(0, 0)
+        vw.append([tile("vw10", [P, BANK], U32, tag="tabs"), tile("vw11", [P, BANK], U32)])
+        gather_table(1)
+        round_w1(1, 1, ("scalar", "vector"))
+        quantize(w1c[0][1], w1s[0][1], wbf[1], pieces=2)
+        first_product(0, 1)
+        features(0)
+        round_w1(2, 0, ("scalar", "scalar"))
+        quantize(w1c[1][0], w1s[1][0], wbf[0])
+        round_w1(3, 1, ("scalar", "vector"))
+        quantize(w1c[1][1], w1s[1][1], wbf[1])
+        load_weight(w3, 0, 0, 0)
+        load_weight(w3, 1, 1, 0)
+        nc.sync.dma_start(
+            out=w4c[:].bitcast(I32), in_=w4_words.rearrange("a p c i -> p a (c i)").bitcast(I32)
+        )
+        for q in range(4):
+            nc.sync.dma_start(
+                out=w4s[32 * q : 32 * q + 4, :].bitcast(I32).rearrange("r (a c) -> r a c", a=PASSES),
+                in_=w4_scales[:, 4 * q : 4 * q + 4, :].bitcast(I32).rearrange("a r c -> r a c"),
+            )
+        first_product(1, 0)
+        first_product(1, 1)
+        features(1)
+        weave("scalar", x1bf[0][:], x1[0][:])
+        quantize(x1c[0], x1s[0], x1bf[0])
+        weave("scalar", x1bf[1][:], x1[1][:])
+        w2c = tile("w2c", [P, PASSES * H], U16, tag="h3")
+        w2s = tile("w2s", [P, PASSES * H], U8, tag="low_sb")
+        nc.vector.tensor_copy(
+            out=w2s[:].rearrange("p (g t m) -> p g t m", g=4, t=PACK),
+            in_=w2sraw[:].rearrange("p (g m t) -> p g t m", g=4, t=PACK),
+        )
+        for a in range(PASSES):
+            nc.vector.tensor_copy(
+                out=w2c[:, H * a : H * (a + 1)].rearrange("p (b t m) -> p b t m", b=2, t=PACK),
+                in_=w2raw[a][:].rearrange("p (b m t) -> p b t m", b=2, t=PACK),
+            )
+        quantize(x1c[1], x1s[1], x1bf[1])
+
+        for i in range(8):
+            for a in range(PASSES):
+                cols = slice(H * a + P * i, H * a + P * (i + 1))
+                nc.tensor.matmul_mx(
+                    out=banks[i][:],
+                    lhsT=w2c[:, cols].bitcast(E2M1),
+                    lhsT_scale=w2s[:, cols],
+                    rhs=x1c[a][:].bitcast(E4M3),
+                    rhs_scale=x1s[a][:],
+                    start=(a == 0),
+                    stop=(a == PASSES - 1),
+                )
+
+        def distance(i):
+            b, t = divmod(i, PACK)
+            nc.vector.tensor_tensor(out=z[i % 4][:], in0=banks[i][:], in1=base_sb[b][:, t, :], op=ALU.subtract)
+            nc.scalar.activation(z[i % 4][:], z[i % 4][:], ACT.Tanh)
+
+        def step(i):
+            b, t = divmod(i, PACK)
+            nc.vector.scalar_tensor_tensor(
+                out=x2[i % 2][:],
+                in0=z[i % 4][:],
+                scalar=gain_sb[:, b, t : t + 1],
+                in1=x1[b][:, t, :],
+                op0=ALU.mult,
+                op1=ALU.add,
+            )
+
+        def pick_x3(i):
+            b, t = divmod(i, PACK)
+            nc.vector.tensor_copy(x3[b][:, t, :], x2[i % 2][:].indirect(pos2_sb[:]))
+
+        def last_products(a):
+            for c in range(4):
+                cols = slice(P * c, P * (c + 1))
+                for k, (codes, scales) in enumerate(
+                    ((w3c[a][:, cols], w3s[a][:, cols]), (w4c[:, a, cols], w4s[:, N * a + P * c : N * a + P * (c + 1)]))
+                ):
+                    nc.tensor.matmul_mx(
+                        out=banks[2 * c + k][:, 0:P2],
+                        lhsT=codes.bitcast(E4M3),
+                        lhsT_scale=scales,
+                        rhs=x3c[a][:].bitcast(E4M3),
+                        rhs_scale=x3s[a][:],
+                        start=(a == 0),
+                        stop=(a == PASSES - 1),
+                    )
+
+        def round_w3(a, f):
+            weave("scalar", wbf[a][:, 1024 * f : 1024 * (f + 1)], raw[a][f][:])
+
+        for i in range(8 + 2):
+            if i < 8:
+                distance(i)
+            if 1 <= i < 9:
+                step(i - 1)
+            if i >= 2:
+                pick_x3(i - 2)
+            if i < 4:
+                round_w3(i // 2, i % 2)
+            if i in (2, 4):
+                quantize(w3c[i // 2 - 1], w3s[i // 2 - 1], wbf[i // 2 - 1])
+            if i == 5:
+                weave("scalar", x3bf[0][:], x3[0][:])
+                quantize(x3c[0], x3s[0], x3bf[0])
+        last_products(0)
+        weave("vector", x3bf[1][:], x3[1][:])
+        quantize(x3c[1], x3s[1], x3bf[1])
+        last_products(1)
+        for c in range(4):
+            nc.scalar.activation(sq[c][:], banks[2 * c][:, 0:P2], ACT.Square)
+            nc.vector.tensor_tensor(out=res[c][:], in0=banks[2 * c + 1][:, 0:P2], in1=sq[c][:], op=ALU.add)
+            nc.sync.dma_start(out=out[P * c : P * (c + 1), :], in_=res[c][:])

@@ -21,6 +21,7 @@ PACK = 4
 PASS = P * PACK
 PASSES = 2
 BANK = 512
+CUT = 384
 
 
 def tile_list_rope_trace_trunk_kernel(
@@ -44,7 +45,8 @@ def tile_list_rope_trace_trunk_kernel(
         tabs = tile("tabs", [P, T], U8)
         vw = [[tile("vw0%d" % f, [P, BANK], U32) for f in range(2)]]
         vs = tile("vs", [P, S], U8)
-        raw = [[tile("raw%d%d" % (i, f), [P, PACK, 256], F32) for f in range(2)] for i in range(4)]
+        raw = [tile("raw%d" % i, [P, PACK, PASS], F32) for i in range(3)]
+        rawh = [tile("rawh%d" % f, [P, PACK, 256], F32) for f in range(2)]
         wbf = [tile("wbf%d" % i, [P, PASS * PACK], BF16) for i in range(2)]
         w1c = [[tile("w1c%d%d" % (b, a), [P, PASS], U32) for a in range(PASSES)] for b in range(2)]
         w1s = [[tile("w1s%d%d" % (b, a), [P, PASS], U8) for a in range(PASSES)] for b in range(2)]
@@ -53,7 +55,7 @@ def tile_list_rope_trace_trunk_kernel(
         x1bf = [tile("x1bf%d" % b, [P, P1 * PACK], BF16) for b in range(2)]
         x1c = [tile("x1c%d" % b, [P, P1], U32) for b in range(2)]
         x1s = [tile("x1s%d" % b, [P, P1], U8) for b in range(2)]
-        w2raw = [tile("w2raw%d" % a, [P, H], U16) for a in range(PASSES)]
+        w2raw = tile("w2raw", [P, PASSES, H], U16)
         w2sraw = tile("w2sraw", [P, PASSES * H], U8)
         base_sb = [tile("base%d" % b, [P, PACK, P1], F32) for b in range(2)]
         low_sb = tile("low_sb", [P, 2, 8], F32)
@@ -77,49 +79,47 @@ def tile_list_rope_trace_trunk_kernel(
         nc.scalar.activation(warm[:, 0:1], warm[:, 4:5], ACT.Tanh)
         nc.vector.memset(w2sraw[:].bitcast(I32), 0)
         nc.vector.memset(w4s[:].bitcast(I32), 0)
-        for q in range(4):
-            nc.gpsimd.dma_start(
-                out=tabs[32 * q : 32 * q + 8, :].bitcast(I32), in_=tab_scales[:, 4 * q : 4 * q + 4, :].bitcast(I32)
-            )
 
         def load_table(a):
             nc.sync.dma_start(
                 out=tabw[a][:].bitcast(I32), in_=tab_words[a].rearrange("p t i -> p (t i)").bitcast(I32)
             )
 
-        def load_weight(w, slot, a, c0):
-            for f in range(2):
-                cols = slice(c0 + 256 * f, c0 + 256 * (f + 1))
-                nc.sync.dma_start(
-                    out=raw[slot][f][:],
-                    in_=w[PASS * a : PASS * (a + 1), cols].rearrange("(p j) c -> p j c", j=PACK),
-                )
+        def load_weight(dst, w, a, c0):
+            cols = slice(c0, c0 + dst.shape[2])
+            nc.sync.dma_start(out=dst[:], in_=w[PASS * a : PASS * (a + 1), cols].rearrange("(p j) c -> p j c", j=PACK))
 
         def load_vector(dst, vec):
             nc.sync.dma_start(out=dst[:, :, 0:PACK], in_=vec.rearrange("(b p t) -> p b t", p=P, t=PACK))
 
-        nc.sync.dma_start(offs_sb[:], offs)
+        def load_base(b):
+            nc.sync.dma_start(
+                out=base_sb[b][:], in_=base[PASS * b : PASS * (b + 1), :].rearrange("(p t) j -> p t j", t=PACK)
+            )
+
         load_table(0)
-        load_weight(w1, 0, 0, 0)
+        nc.sync.dma_start(offs_sb[:], offs)
+        for q in range(4):
+            nc.sync.dma_start(
+                out=tabs[32 * q : 32 * q + 8, :].bitcast(I32), in_=tab_scales[:, 4 * q : 4 * q + 4, :].bitcast(I32)
+            )
+        load_weight(raw[0], w1, 0, 0)
         load_table(1)
-        load_weight(w1, 1, 1, 0)
+        load_weight(rawh[0], w1, 1, 0)
+        load_weight(rawh[1], w1, 1, 256)
         nc.sync.dma_start(pos1_sb[:], pos1)
         load_vector(low_sb, low)
-        load_weight(w1, 2, 0, PASS)
-        load_weight(w1, 3, 1, PASS)
-        for a in range(PASSES):
-            nc.sync.dma_start(out=w2raw[a][:].bitcast(I32), in_=w2_words[a].bitcast(I32))
+        load_weight(raw[1], w1, 0, PASS)
+        load_weight(raw[2], w1, 1, PASS)
+        nc.sync.dma_start(out=w2raw[:].bitcast(I32), in_=w2_words.rearrange("a p c -> p a c").bitcast(I32))
         for q in range(4):
             nc.sync.dma_start(
                 out=w2sraw[32 * q : 32 * q + 4, :].bitcast(I32).rearrange("r (a c) -> r a c", a=PASSES),
                 in_=w2_scales[:, 4 * q : 4 * q + 4, :].bitcast(I32).rearrange("a r c -> r a c"),
             )
+        load_base(0)
         load_vector(gain_sb, gain)
         nc.sync.dma_start(pos2_sb[:], pos2)
-        for b in range(2):
-            nc.sync.dma_start(
-                out=base_sb[b][:], in_=base[PASS * b : PASS * (b + 1), :].rearrange("(p t) j -> p t j", t=PACK)
-            )
 
         def copy_on(engine, dst, src):
             if engine == "vector":
@@ -127,14 +127,10 @@ def tile_list_rope_trace_trunk_kernel(
             else:
                 nc.scalar.copy(out=dst, in_=src)
 
-        def round_w1(slot, stage, engines):
+        def round_w1(engine, stage, src, c0):
             dealt = wbf[stage][:].rearrange("p (t m j) -> p m j t", t=PACK, j=PACK)
-            for f in range(2):
-                copy_on(
-                    engines[f],
-                    dealt[:, 64 * f : 64 * (f + 1)],
-                    raw[slot][f][:].rearrange("p j (m t) -> p m j t", t=PACK),
-                )
+            m0, m1 = c0 // PACK, (c0 + src.shape[2]) // PACK
+            copy_on(engine, dealt[:, m0:m1], src.rearrange("p j (m t) -> p m j t", t=PACK))
 
         def weave(engine, dst, src):
             copy_on(
@@ -157,57 +153,55 @@ def tile_list_rope_trace_trunk_kernel(
             for f in range(2):
                 nc.vector.tensor_copy(vw[a][f][:], tabw[a][:].indirect(offs_sb[:, 32 * f : 32 * (f + 1)]))
 
-        def first_product(b, a):
-            for t in range(PACK):
-                cols = slice(P * t, P * (t + 1))
-                for f in range(2):
-                    nc.tensor.matmul_mx(
-                        out=banks[2 * t + f][:],
-                        lhsT=w1c[b][a][:, cols].bitcast(E4M3),
-                        lhsT_scale=w1s[b][a][:, cols],
-                        rhs=vw[a][f][:].bitcast(E4M3),
-                        rhs_scale=vs[4 * a : P, BANK * f : BANK * (f + 1)],
-                        start=(a == 0),
-                        stop=(a == PASSES - 1),
-                    )
-
-        def evacuate_h(t):
+        def first_product(b, t, a):
+            cols = slice(P * t, P * (t + 1))
             for f in range(2):
-                nc.scalar.copy(out=h[t][:, BANK * f : BANK * (f + 1)], in_=banks[2 * t + f][:])
+                nc.tensor.matmul_mx(
+                    out=banks[2 * t + f][:],
+                    lhsT=w1c[b][a][:, cols].bitcast(E4M3),
+                    lhsT_scale=w1s[b][a][:, cols],
+                    rhs=vw[a][f][:].bitcast(E4M3),
+                    rhs_scale=vs[4 * a : P, BANK * f : BANK * (f + 1)],
+                    start=(a == 0),
+                    stop=(a == PASSES - 1),
+                )
 
-        def pick_x1(b, t):
-            nc.vector.tensor_copy(x1[b][:, t, :], h[t][:].indirect(pos1_sb[:]))
-
-        def floor_x1(b, t):
-            nc.vector.tensor_scalar(
-                out=x1[b][:, t, :], in0=x1[b][:, t, :], scalar1=low_sb[:, b, t : t + 1], scalar2=None, op0=ALU.max
-            )
-
-        def features(b):
-            for t in range(PACK):
-                evacuate_h(t)
-                pick_x1(b, t)
-                if t > 0:
-                    floor_x1(b, t - 1)
-            floor_x1(b, PACK - 1)
+        def features(b, t, engines=("scalar", "scalar")):
+            for f in range(2):
+                copy_on(engines[f], h[t][:, BANK * f : BANK * (f + 1)], banks[2 * t + f][:])
+            halves = [x1[b][:, t, 256 * f : 256 * (f + 1)] for f in range(2)]
+            for f in range(2):
+                nc.vector.tensor_copy(halves[f], h[t][:].indirect(pos1_sb[:, 16 * f : 16 * (f + 1)]))
+            for f in range(2):
+                nc.vector.tensor_scalar(
+                    out=halves[f], in0=halves[f], scalar1=low_sb[:, b, t : t + 1], scalar2=None, op0=ALU.max
+                )
 
         gather_table(0)
-        round_w1(0, 0, ("scalar", "scalar"))
+        round_w1("scalar", 0, raw[0][:], 0)
         nc.vector.tensor_copy(vs[:], tabs[:].indirect(offs_sb[:]))
         quantize(w1c[0][0], w1s[0][0], wbf[0])
-        first_product(0, 0)
+        for t in range(PACK):
+            first_product(0, t, 0)
         vw.append([tile("vw10", [P, BANK], U32, tag="tabs"), tile("vw11", [P, BANK], U32)])
         gather_table(1)
-        round_w1(1, 1, ("scalar", "vector"))
+        round_w1("scalar", 1, rawh[0][:], 0)
+        round_w1("vector", 1, rawh[1][:], 256)
         quantize(w1c[0][1], w1s[0][1], wbf[1], pieces=2)
-        first_product(0, 1)
-        features(0)
-        round_w1(2, 0, ("scalar", "scalar"))
+        for t in range(PACK):
+            first_product(0, t, 1)
+        features(0, 0, ("scalar", "vector"))
+        features(0, 1)
+        round_w1("scalar", 0, raw[1][:], 0)
+        round_w1("vector", 1, raw[2][:, :, 0:CUT], 0)
+        round_w1("scalar", 1, raw[2][:, :, CUT:512], CUT)
         quantize(w1c[1][0], w1s[1][0], wbf[0])
-        round_w1(3, 1, ("scalar", "vector"))
         quantize(w1c[1][1], w1s[1][1], wbf[1])
-        load_weight(w3, 0, 0, 0)
-        load_weight(w3, 1, 1, 0)
+        features(0, 2)
+        features(0, 3)
+        load_weight(raw[0], w3, 0, 0)
+        load_base(1)
+        load_weight(raw[1], w3, 1, 0)
         nc.sync.dma_start(
             out=w4c[:].bitcast(I32), in_=w4_words.rearrange("a p c i -> p a (c i)").bitcast(I32)
         )
@@ -216,32 +210,45 @@ def tile_list_rope_trace_trunk_kernel(
                 out=w4s[32 * q : 32 * q + 4, :].bitcast(I32).rearrange("r (a c) -> r a c", a=PASSES),
                 in_=w4_scales[:, 4 * q : 4 * q + 4, :].bitcast(I32).rearrange("a r c -> r a c"),
             )
-        first_product(1, 0)
-        first_product(1, 1)
-        features(1)
-        weave("scalar", x1bf[0][:], x1[0][:])
-        quantize(x1c[0], x1s[0], x1bf[0])
-        weave("scalar", x1bf[1][:], x1[1][:])
-        w2c = tile("w2c", [P, PASSES * H], U16, tag="h3")
-        w2s = tile("w2s", [P, PASSES * H], U8, tag="low_sb")
-        nc.vector.tensor_copy(
-            out=w2s[:].rearrange("p (g t m) -> p g t m", g=4, t=PACK),
-            in_=w2sraw[:].rearrange("p (g m t) -> p g t m", g=4, t=PACK),
-        )
-        for a in range(PASSES):
+        w2c, w2s = [], []
+
+        def deal_w2(b, words_tag, scales_tag):
+            w2s.append(tile("w2s%d" % b, [P, PASSES, PASS], U8, tag=scales_tag))
+            w2c.append(tile("w2c%d" % b, [P, PASSES, PASS], U16, tag=words_tag))
             nc.vector.tensor_copy(
-                out=w2c[:, H * a : H * (a + 1)].rearrange("p (b t m) -> p b t m", b=2, t=PACK),
-                in_=w2raw[a][:].rearrange("p (b m t) -> p b t m", b=2, t=PACK),
+                out=w2s[b][:].rearrange("p a (t m) -> p a t m", t=PACK),
+                in_=w2sraw[:].rearrange("p (a b m t) -> p b a t m", a=PASSES, b=2, t=PACK)[:, b],
             )
+            nc.vector.tensor_copy(
+                out=w2c[b][:].rearrange("p a (t m) -> p a t m", t=PACK),
+                in_=w2raw[:].rearrange("p a (b m t) -> p b a t m", b=2, t=PACK)[:, b],
+            )
+
+        for t in range(PACK):
+            for a in range(PASSES):
+                first_product(1, t, a)
+        features(1, 0)
+        features(1, 1)
+        weave("scalar", x1bf[0][:, 0:1024], x1[0][:, :, 0:256])
+        features(1, 2)
+        weave("scalar", x1bf[0][:, 1024:2048], x1[0][:, :, 256:512])
+        deal_w2(0, "h1", "w2s0")
+        quantize(x1c[0], x1s[0], x1bf[0])
+        features(1, 3)
+        split = 256
+        weave("scalar", x1bf[1][:, 0 : PACK * split], x1[1][:, :, 0:split])
+        weave("vector", x1bf[1][:, PACK * split :], x1[1][:, :, split:])
         quantize(x1c[1], x1s[1], x1bf[1])
+        deal_w2(1, "x1bf1", "low_sb")
 
         for i in range(8):
+            b, t = divmod(i, PACK)
+            cols = slice(P * t, P * (t + 1))
             for a in range(PASSES):
-                cols = slice(H * a + P * i, H * a + P * (i + 1))
                 nc.tensor.matmul_mx(
                     out=banks[i][:],
-                    lhsT=w2c[:, cols].bitcast(E2M1),
-                    lhsT_scale=w2s[:, cols],
+                    lhsT=w2c[b][:, a, cols].bitcast(E2M1),
+                    lhsT_scale=w2s[b][:, a, cols],
                     rhs=x1c[a][:].bitcast(E4M3),
                     rhs_scale=x1s[a][:],
                     start=(a == 0),
@@ -285,7 +292,7 @@ def tile_list_rope_trace_trunk_kernel(
                     )
 
         def round_w3(a, f):
-            weave("scalar", wbf[a][:, 1024 * f : 1024 * (f + 1)], raw[a][f][:])
+            weave("scalar", wbf[a][:, 1024 * f : 1024 * (f + 1)], raw[a][:, :, 256 * f : 256 * (f + 1)])
 
         for i in range(8 + 2):
             if i < 8:

@@ -21,6 +21,8 @@ PACK = 4
 PASS = P * PACK
 PASSES = 2
 BANK = 512
+X3TAG = "z2"
+X3CUT = 64
 CUT = 384
 
 
@@ -64,7 +66,6 @@ def tile_list_rope_trace_trunk_kernel(
         x2 = [tile("x2_%d" % i, [P, P1], F32) for i in range(2)]
         x3 = [tile("x3_%d" % b, [P, PACK, P2], F32) for b in range(2)]
         x3bf = [tile("x3bf%d" % b, [P, P2 * PACK], BF16) for b in range(2)]
-        x3c = [tile("x3c%d" % b, [P, P2], U32) for b in range(2)]
         x3s = [tile("x3s%d" % b, [P, P2], U8) for b in range(2)]
         w3c = [tile("w3c%d" % a, [P, N], U32) for a in range(PASSES)]
         w3s = [tile("w3s%d" % a, [P, N], U8) for a in range(PASSES)]
@@ -72,13 +73,14 @@ def tile_list_rope_trace_trunk_kernel(
         w4s = tile("w4s", [P, PASSES * N], U8)
         sq = [tile("sq%d" % i, [P, P2], F32) for i in range(4)]
         res = [tile("res%d" % i, [P, P2], F32) for i in range(4)]
-        warm = tile("warm", [P, 8], F32)
 
         nc.vector.memset(tabs[:].bitcast(I32), 0)
-        nc.vector.memset(warm[:], 0.0)
-        nc.scalar.activation(warm[:, 0:1], warm[:, 4:5], ACT.Tanh)
         nc.vector.memset(w2sraw[:].bitcast(I32), 0)
         nc.vector.memset(w4s[:].bitcast(I32), 0)
+        for q in range(4):
+            nc.gpsimd.dma_start(
+                out=tabs[32 * q : 32 * q + 8, :].bitcast(I32), in_=tab_scales[:, 4 * q : 4 * q + 4, :].bitcast(I32)
+            )
 
         def load_table(a):
             nc.sync.dma_start(
@@ -99,16 +101,12 @@ def tile_list_rope_trace_trunk_kernel(
 
         load_table(0)
         nc.sync.dma_start(offs_sb[:], offs)
-        for q in range(4):
-            nc.sync.dma_start(
-                out=tabs[32 * q : 32 * q + 8, :].bitcast(I32), in_=tab_scales[:, 4 * q : 4 * q + 4, :].bitcast(I32)
-            )
         load_weight(raw[0], w1, 0, 0)
+        nc.sync.dma_start(pos1_sb[:], pos1)
+        load_vector(low_sb, low)
         load_table(1)
         load_weight(rawh[0], w1, 1, 0)
         load_weight(rawh[1], w1, 1, 256)
-        nc.sync.dma_start(pos1_sb[:], pos1)
-        load_vector(low_sb, low)
         load_weight(raw[1], w1, 0, PASS)
         load_weight(raw[2], w1, 1, PASS)
         nc.sync.dma_start(out=w2raw[:].bitcast(I32), in_=w2_words.rearrange("a p c -> p a c").bitcast(I32))
@@ -128,15 +126,15 @@ def tile_list_rope_trace_trunk_kernel(
                 nc.scalar.copy(out=dst, in_=src)
 
         def round_w1(engine, stage, src, c0):
-            dealt = wbf[stage][:].rearrange("p (t m j) -> p m j t", t=PACK, j=PACK)
+            dealt = wbf[stage][:].rearrange("p (u e m j) -> p u m j e", u=2, e=2, j=PACK)
             m0, m1 = c0 // PACK, (c0 + src.shape[2]) // PACK
-            copy_on(engine, dealt[:, m0:m1], src.rearrange("p j (m t) -> p m j t", t=PACK))
+            copy_on(engine, dealt[:, :, m0:m1], src.rearrange("p j (m u e) -> p u m j e", u=2, e=2))
 
         def weave(engine, dst, src):
             copy_on(
                 engine,
-                dst.rearrange("p (c i t) -> p c t i", i=4, t=PACK),
-                src.rearrange("p t (c i) -> p c t i", i=4),
+                dst.rearrange("p (c i t) -> p c t i", i=2, t=PACK),
+                src.rearrange("p t (c i) -> p c t i", i=2),
             )
 
         def quantize(codes, scales, src, pieces=1):
@@ -168,7 +166,11 @@ def tile_list_rope_trace_trunk_kernel(
 
         def features(b, t, engines=("scalar", "scalar")):
             for f in range(2):
-                copy_on(engines[f], h[t][:, BANK * f : BANK * (f + 1)], banks[2 * t + f][:])
+                dst = h[t][:, BANK * f : BANK * (f + 1)]
+                if engines[f] == "vector":
+                    nc.vector.tensor_copy(out=dst, in_=banks[2 * t + f][:])
+                else:
+                    nc.scalar.activation(dst, banks[2 * t + f][:], ACT.Copy)
             halves = [x1[b][:, t, 256 * f : 256 * (f + 1)] for f in range(2)]
             for f in range(2):
                 nc.vector.tensor_copy(halves[f], h[t][:].indirect(pos1_sb[:, 16 * f : 16 * (f + 1)]))
@@ -307,9 +309,12 @@ def tile_list_rope_trace_trunk_kernel(
                 quantize(w3c[i // 2 - 1], w3s[i // 2 - 1], wbf[i // 2 - 1])
             if i == 5:
                 weave("scalar", x3bf[0][:], x3[0][:])
+            if i == 8:
+                x3c = [tile("x3c0", [P, P2], U32, tag=X3TAG), tile("x3c1", [P, P2], U32)]
                 quantize(x3c[0], x3s[0], x3bf[0])
         last_products(0)
-        weave("vector", x3bf[1][:], x3[1][:])
+        weave("vector", x3bf[1][:, PACK * X3CUT :], x3[1][:, :, X3CUT:])
+        weave("scalar", x3bf[1][:, 0 : PACK * X3CUT], x3[1][:, :, 0:X3CUT])
         quantize(x3c[1], x3s[1], x3bf[1])
         last_products(1)
         for c in range(4):

from contextlib import ExitStack

import concourse.mybir as mybir

K, H, N, T, S, P1, P2 = 1024, 1024, 512, 4096, 1024, 512, 256
FLOPS = 2 * (K * H * S + H * H * P1 + 2 * H * N * P2)

F32 = mybir.dt.float32
BF16 = mybir.dt.bfloat16
I32 = mybir.dt.int32
U32 = mybir.dt.uint32
U16 = mybir.dt.uint16
U8 = mybir.dt.uint8
E4M3 = mybir.dt.float8_e4m3fn_x4
E2M1 = mybir.dt.float4_e2m1fn_x4
ALU = mybir.AluOpType
ACT = mybir.ActivationFunctionType

P = 128
PACK = 4
PASS = P * PACK
PASSES = 2
BANK = 512
X3TAG = "z2"
X3CUT = 64
CUT = 384


def tile_list_rope_trace_trunk_kernel(
    tc, tab_words, tab_scales, offs, pos1, pos2, w1, low, w2_words, w2_scales, base, gain, w3, w4_words, w4_scales, out
):
    nc = tc.nc
    with ExitStack() as ctx:
        sb = ctx.enter_context(tc.tile_pool(name="sb", bufs=1))
        ps = ctx.enter_context(tc.psum_pool(name="ps", bufs=1))

        def tile(name, shape, dtype, tag=None):
            return sb.tile(shape, dtype, name=name, tag=tag or name, align_bytes=64)

        banks = [ps.tile([P, BANK], F32, name="bank%d" % i) for i in range(8)]

        offs_sb = sb.tile([P, S // 16], U16, name="offs_sb")
        pos1_sb = sb.tile([P, P1 // 16], U16, name="pos1_sb")
        pos2_sb = sb.tile([P, P2 // 16], U16, name="pos2_sb")

        tabw = [tile("tabw%d" % a, [P, T], U32) for a in range(PASSES)]
        tabs = tile("tabs", [P, T], U8)
        vw = [[tile("vw0%d" % f, [P, BANK], U32) for f in range(2)]]
        vs = tile("vs", [P, S], U8)
        raw = [tile("raw%d" % i, [P, PACK, PASS], F32) for i in range(3)]
        rawh = [tile("rawh%d" % f, [P, PACK, 256], F32) for f in range(2)]
        wbf = [tile("wbf%d" % i, [P, PASS * PACK], BF16) for i in range(2)]
        w1c = [[tile("w1c%d%d" % (b, a), [P, PASS], U32) for a in range(PASSES)] for b in range(2)]
        w1s = [[tile("w1s%d%d" % (b, a), [P, PASS], U8) for a in range(PASSES)] for b in range(2)]
        h = [tile("h%d" % t, [P, S], F32) for t in range(PACK)]
        x1 = [tile("x1_%d" % b, [P, PACK, P1], F32) for b in range(2)]
        x1bf = [tile("x1bf%d" % b, [P, P1 * PACK], BF16) for b in range(2)]
        x1c = [tile("x1c%d" % b, [P, P1], U32) for b in range(2)]
        x1s = [tile("x1s%d" % b, [P, P1], U8) for b in range(2)]
        w2raw = tile("w2raw", [P, PASSES, H], U16)
        w2sraw = tile("w2sraw", [P, PASSES * H], U8)
        base_sb = [tile("base%d" % b, [P, PACK, P1], F32) for b in range(2)]
        low_sb = tile("low_sb", [P, 2, 8], F32)
        gain_sb = tile("gain_sb", [P, 2, 8], F32)
        z = [tile("z%d" % i, [P, P1], F32) for i in range(4)]
        x2 = [tile("x2_%d" % i, [P, P1], F32) for i in range(2)]
        x3 = [tile("x3_%d" % b, [P, PACK, P2], F32) for b in range(2)]
        x3bf = [tile("x3bf%d" % b, [P, P2 * PACK], BF16) for b in range(2)]
        x3s = [tile("x3s%d" % b, [P, P2], U8) for b in range(2)]
        w3c = [tile("w3c%d" % a, [P, N], U32) for a in range(PASSES)]
        w3s = [tile("w3s%d" % a, [P, N], U8) for a in range(PASSES)]
        w4c = tile("w4c", [P, PASSES, N], U32)
        w4s = tile("w4s", [P, PASSES * N], U8)
        sq = [tile("sq%d" % i, [P, P2], F32) for i in range(4)]
        res = [tile("res%d" % i, [P, P2], F32) for i in range(4)]

        nc.vector.memset(tabs[:].bitcast(I32), 0)
        nc.vector.memset(w2sraw[:].bitcast(I32), 0)
        nc.vector.memset(w4s[:].bitcast(I32), 0)
        for q in range(4):
            nc.gpsimd.dma_start(
                out=tabs[32 * q : 32 * q + 8, :].bitcast(I32), in_=tab_scales[:, 4 * q : 4 * q + 4, :].bitcast(I32)
            )

        def load_table(a):
            nc.sync.dma_start(
                out=tabw[a][:].bitcast(I32), in_=tab_words[a].rearrange("p t i -> p (t i)").bitcast(I32)
            )

        def load_weight(dst, w, a, c0):
            cols = slice(c0, c0 + dst.shape[2])
            nc.sync.dma_start(out=dst[:], in_=w[PASS * a : PASS * (a + 1), cols].rearrange("(p j) c -> p j c", j=PACK))

        def load_vector(dst, vec):
            nc.sync.dma_start(out=dst[:, :, 0:PACK], in_=vec.rearrange("(b p t) -> p b t", p=P, t=PACK))

        def load_base(b):
            nc.sync.dma_start(
                out=base_sb[b][:], in_=base[PASS * b : PASS * (b + 1), :].rearrange("(p t) j -> p t j", t=PACK)
            )

        load_table(0)
        nc.sync.dma_start(offs_sb[:], offs)
        load_weight(raw[0], w1, 0, 0)
        nc.sync.dma_start(pos1_sb[:], pos1)
        load_vector(low_sb, low)
        load_table(1)
        load_weight(rawh[0], w1, 1, 0)
        load_weight(rawh[1], w1, 1, 256)
        load_weight(raw[1], w1, 0, PASS)
        load_weight(raw[2], w1, 1, PASS)
        nc.sync.dma_start(out=w2raw[:].bitcast(I32), in_=w2_words.rearrange("a p c -> p a c").bitcast(I32))
        for q in range(4):
            nc.sync.dma_start(
                out=w2sraw[32 * q : 32 * q + 4, :].bitcast(I32).rearrange("r (a c) -> r a c", a=PASSES),
                in_=w2_scales[:, 4 * q : 4 * q + 4, :].bitcast(I32).rearrange("a r c -> r a c"),
            )
        load_base(0)
        load_vector(gain_sb, gain)
        nc.sync.dma_start(pos2_sb[:], pos2)

        def copy_on(engine, dst, src):
            if engine == "vector":
                nc.vector.tensor_copy(out=dst, in_=src)
            else:
                nc.scalar.copy(out=dst, in_=src)

        def round_w1(engine, stage, src, c0):
            dealt = wbf[stage][:].rearrange("p (u e m j) -> p u m j e", u=2, e=2, j=PACK)
            m0, m1 = c0 // PACK, (c0 + src.shape[2]) // PACK
            copy_on(engine, dealt[:, :, m0:m1], src.rearrange("p j (m u e) -> p u m j e", u=2, e=2))

        def weave(engine, dst, src):
            copy_on(
                engine,
                dst.rearrange("p (c i t) -> p c t i", i=2, t=PACK),
                src.rearrange("p t (c i) -> p c t i", i=2),
            )

        def quantize(codes, scales, src, pieces=1):
            width = codes.shape[1] // pieces
            for i in range(pieces):
                cols = slice(i * width, (i + 1) * width)
                nc.vector.quantize_mx(
                    out=codes[:, cols].bitcast(E4M3),
                    scales=scales[:, cols],
                    in_=src[:, PACK * i * width : PACK * (i + 1) * width],
                )

        def gather_table(a):
            for f in range(2):
                nc.vector.tensor_copy(vw[a][f][:], tabw[a][:].indirect(offs_sb[:, 32 * f : 32 * (f + 1)]))

        def first_product(b, t, a):
            cols = slice(P * t, P * (t + 1))
            for f in range(2):
                nc.tensor.matmul_mx(
                    out=banks[2 * t + f][:],
                    lhsT=w1c[b][a][:, cols].bitcast(E4M3),
                    lhsT_scale=w1s[b][a][:, cols],
                    rhs=vw[a][f][:].bitcast(E4M3),
                    rhs_scale=vs[4 * a : P, BANK * f : BANK * (f + 1)],
                    start=(a == 0),
                    stop=(a == PASSES - 1),
                )

        def features(b, t, engines=("scalar", "scalar")):
            for f in range(2):
                dst = h[t][:, BANK * f : BANK * (f + 1)]
                if engines[f] == "vector":
                    nc.vector.tensor_copy(out=dst, in_=banks[2 * t + f][:])
                else:
                    nc.scalar.activation(dst, banks[2 * t + f][:], ACT.Copy)
            halves = [x1[b][:, t, 256 * f : 256 * (f + 1)] for f in range(2)]
            for f in range(2):
                nc.vector.tensor_copy(halves[f], h[t][:].indirect(pos1_sb[:, 16 * f : 16 * (f + 1)]))
            for f in range(2):
                nc.vector.tensor_scalar(
                    out=halves[f], in0=halves[f], scalar1=low_sb[:, b, t : t + 1], scalar2=None, op0=ALU.max
                )

        gather_table(0)
        round_w1("scalar", 0, raw[0][:], 0)
        nc.vector.tensor_copy(vs[:], tabs[:].indirect(offs_sb[:]))
        quantize(w1c[0][0], w1s[0][0], wbf[0])
        for t in range(PACK):
            first_product(0, t, 0)
        vw.append([tile("vw10", [P, BANK], U32, tag="tabs"), tile("vw11", [P, BANK], U32)])
        gather_table(1)
        round_w1("scalar", 1, rawh[0][:], 0)
        round_w1("vector", 1, rawh[1][:], 256)
        quantize(w1c[0][1], w1s[0][1], wbf[1], pieces=2)
        for t in range(PACK):
            first_product(0, t, 1)
        features(0, 0, ("scalar", "vector"))
        features(0, 1)
        round_w1("scalar", 0, raw[1][:], 0)
        round_w1("vector", 1, raw[2][:, :, 0:CUT], 0)
        round_w1("scalar", 1, raw[2][:, :, CUT:512], CUT)
        quantize(w1c[1][0], w1s[1][0], wbf[0])
        quantize(w1c[1][1], w1s[1][1], wbf[1])
        features(0, 2)
        features(0, 3)
        load_weight(raw[0], w3, 0, 0)
        load_base(1)
        load_weight(raw[1], w3, 1, 0)
        nc.sync.dma_start(
            out=w4c[:].bitcast(I32), in_=w4_words.rearrange("a p c i -> p a (c i)").bitcast(I32)
        )
        for q in range(4):
            nc.sync.dma_start(
                out=w4s[32 * q : 32 * q + 4, :].bitcast(I32).rearrange("r (a c) -> r a c", a=PASSES),
                in_=w4_scales[:, 4 * q : 4 * q + 4, :].bitcast(I32).rearrange("a r c -> r a c"),
            )
        w2c, w2s = [], []

        def deal_w2(b, words_tag, scales_tag):
            w2s.append(tile("w2s%d" % b, [P, PASSES, PASS], U8, tag=scales_tag))
            w2c.append(tile("w2c%d" % b, [P, PASSES, PASS], U16, tag=words_tag))
            nc.vector.tensor_copy(
                out=w2s[b][:].rearrange("p a (t m) -> p a t m", t=PACK),
                in_=w2sraw[:].rearrange("p (a b m t) -> p b a t m", a=PASSES, b=2, t=PACK)[:, b],
            )
            nc.vector.tensor_copy(
                out=w2c[b][:].rearrange("p a (t m) -> p a t m", t=PACK),
                in_=w2raw[:].rearrange("p a (b m t) -> p b a t m", b=2, t=PACK)[:, b],
            )

        for t in range(PACK):
            for a in range(PASSES):
                first_product(1, t, a)
        features(1, 0)
        features(1, 1)
        weave("scalar", x1bf[0][:, 0:1024], x1[0][:, :, 0:256])
        features(1, 2)
        weave("scalar", x1bf[0][:, 1024:2048], x1[0][:, :, 256:512])
        deal_w2(0, "h1", "w2s0")
        quantize(x1c[0], x1s[0], x1bf[0])
        features(1, 3)
        split = 256
        weave("scalar", x1bf[1][:, 0 : PACK * split], x1[1][:, :, 0:split])
        weave("vector", x1bf[1][:, PACK * split :], x1[1][:, :, split:])
        quantize(x1c[1], x1s[1], x1bf[1])
        deal_w2(1, "x1bf1", "low_sb")

        for i in range(8):
            b, t = divmod(i, PACK)
            cols = slice(P * t, P * (t + 1))
            for a in range(PASSES):
                nc.tensor.matmul_mx(
                    out=banks[i][:],
                    lhsT=w2c[b][:, a, cols].bitcast(E2M1),
                    lhsT_scale=w2s[b][:, a, cols],
                    rhs=x1c[a][:].bitcast(E4M3),
                    rhs_scale=x1s[a][:],
                    start=(a == 0),
                    stop=(a == PASSES - 1),
                )

        def distance(i):
            b, t = divmod(i, PACK)
            nc.vector.tensor_tensor(out=z[i % 4][:], in0=banks[i][:], in1=base_sb[b][:, t, :], op=ALU.subtract)
            nc.scalar.activation(z[i % 4][:], z[i % 4][:], ACT.Tanh)

        def step(i):
            b, t = divmod(i, PACK)
            nc.vector.scalar_tensor_tensor(
                out=x2[i % 2][:],
                in0=z[i % 4][:],
                scalar=gain_sb[:, b, t : t + 1],
                in1=x1[b][:, t, :],
                op0=ALU.mult,
                op1=ALU.add,
            )

        def pick_x3(i):
            b, t = divmod(i, PACK)
            nc.vector.tensor_copy(x3[b][:, t, :], x2[i % 2][:].indirect(pos2_sb[:]))

        def last_products(a):
            for c in range(4):
                cols = slice(P * c, P * (c + 1))
                for k, (codes, scales) in enumerate(
                    ((w3c[a][:, cols], w3s[a][:, cols]), (w4c[:, a, cols], w4s[:, N * a + P * c : N * a + P * (c + 1)]))
                ):
                    nc.tensor.matmul_mx(
                        out=banks[2 * c + k][:, 0:P2],
                        lhsT=codes.bitcast(E4M3),
                        lhsT_scale=scales,
                        rhs=x3c[a][:].bitcast(E4M3),
                        rhs_scale=x3s[a][:],
                        start=(a == 0),
                        stop=(a == PASSES - 1),
                    )

        def round_w3(a, f):
            weave("scalar", wbf[a][:, 1024 * f : 1024 * (f + 1)], raw[a][:, :, 256 * f : 256 * (f + 1)])

        for i in range(8 + 2):
            if i < 8:
                distance(i)
            if 1 <= i < 9:
                step(i - 1)
            if i >= 2:
                pick_x3(i - 2)
            if i < 4:
                round_w3(i // 2, i % 2)
            if i in (2, 4):
                quantize(w3c[i // 2 - 1], w3s[i // 2 - 1], wbf[i // 2 - 1])
            if i == 5:
                weave("scalar", x3bf[0][:], x3[0][:])
            if i == 8:
                x3c = [tile("x3c0", [P, P2], U32, tag=X3TAG), tile("x3c1", [P, P2], U32)]
                quantize(x3c[0], x3s[0], x3bf[0])
        last_products(0)
        weave("vector", x3bf[1][:, PACK * X3CUT :], x3[1][:, :, X3CUT:])
        weave("scalar", x3bf[1][:, 0 : PACK * X3CUT], x3[1][:, :, 0:X3CUT])
        quantize(x3c[1], x3s[1], x3bf[1])
        last_products(1)
        for c in range(4):
            nc.scalar.activation(sq[c][:], banks[2 * c][:, 0:P2], ACT.Square)
            nc.vector.tensor_tensor(out=res[c][:], in0=banks[2 * c + 1][:, 0:P2], in1=sq[c][:], op=ALU.add)
            nc.sync.dma_start(out=out[P * c : P * (c + 1), :], in_=res[c][:])
